import numpy as np
import ml_dtypes


def mxq(x, axis, fmt="e4m3"):
    dtype, down = {"e4m3": (ml_dtypes.float8_e4m3fn, 7), "e5m2": (ml_dtypes.float8_e5m2, 14)}[fmt]
    v = np.moveaxis(np.asarray(x, np.float32).astype(ml_dtypes.bfloat16).astype(np.float64), axis, -1)
    blocks = v.reshape(v.shape[:-1] + (-1, 32))
    amax = np.abs(blocks).max(-1, keepdims=True)
    byte = np.maximum(np.where(amax > 0, np.frexp(amax)[1] - 1 + 127, 0) - down, 1)
    scale = np.exp2(byte - 127.0)
    codes = (blocks / scale).astype(np.float32).astype(dtype).astype(np.float64)
    return np.moveaxis((codes * scale).reshape(v.shape), -1, axis)


WIDE = False


def mx_kscale(k):
    if not WIDE:
        return np.ones(k)
    levels = np.array([10, -10, 5, -5, 0])
    if k % 512:
        return np.exp2(np.random.permutation(np.resize(levels, k // 32))).repeat(32)
    a = np.empty((k // 512, 16))
    for p in range(k // 512):
        a[p, :8] = np.random.permutation(np.resize(levels, 8))
        for g in range(8):
            far = levels[np.abs(levels - a[p, g]) >= 10]
            a[p, g + 8] = far[np.random.randint(len(far))]
    return np.exp2(a.ravel()).repeat(32)


def f64(x):
    return np.asarray(x).astype(np.float64)


def striped(idx):
    return np.tile(np.asarray(idx).reshape(-1, 16).T, (8, 1)).astype(np.uint16)


def unstriped(offs):
    return offs[:16].T.reshape(-1).astype(np.int64)


E2M1 = np.array([0.0, 0.5, 1.0, 1.5, 2.0, 3.0, 4.0, 6.0, -0.0, -0.5, -1.0, -1.5, -2.0, -3.0, -4.0, -6.0])


def pack_weight(w, fmt):
    k, n = w.shape
    w = f64(np.asarray(w, np.float32).astype(ml_dtypes.bfloat16)).reshape(k // 32, 32, n)
    amax = np.abs(w).max(1)
    if fmt == "e4m3":
        byte = np.frexp(amax)[1] - 1 + 127 - 7
    else:
        mant, ex = np.frexp(amax / 6.0)
        byte = np.where(mant > 0.5, ex, ex - 1) + 127
    byte = np.clip(np.where(amax > 0, byte, 1), 1, 254)
    scaled = (w * np.exp2(127.0 - byte)[:, None, :]).reshape(k, n).astype(np.float32)
    by_word = np.ascontiguousarray(scaled.reshape(k // 512, 128, 4, n).transpose(0, 1, 3, 2))
    if fmt == "e4m3":
        words = by_word.astype(ml_dtypes.float8_e4m3fn).view(np.uint8)
    else:
        c = by_word.astype(ml_dtypes.float4_e2m1fn).view(np.uint8) & 0xF
        words = (c[..., 0::2] | (c[..., 1::2] << 4)).reshape(k // 512, 128, 2 * n)
    return np.ascontiguousarray(words), np.ascontiguousarray(byte.astype(np.uint8).reshape(k // 512, 16, n))


def unpack_weight(words, scales, fmt):
    g, _, n = scales.shape
    words = np.ascontiguousarray(words).reshape(g, 128, n, -1)
    if fmt == "e4m3":
        vals = words.view(ml_dtypes.float8_e4m3fn).astype(np.float64)
    else:
        nib = np.empty((g, 128, n, 4), np.uint8)
        nib[..., 0::2] = words & 0xF
        nib[..., 1::2] = words >> 4
        vals = E2M1[nib]
    vals = vals * np.repeat(np.exp2(scales.astype(np.float64) - 127.0), 8, axis=1)[..., None]
    return vals.transpose(0, 1, 3, 2).reshape(g * 512, n)


D, E, T, I, Q = 512, 512, 2048, 512, 128


def setup_inputs():
    n = np.random.standard_normal
    idx = np.random.permutation(T)[:I]
    fd = mx_kscale(D)
    fi = mx_kscale(I)
    ti = np.ones(T)
    ti[idx] = fi
    keysp = pack_weight(n((D, T)) / fd[:, None], "e2m1")
    return {
        "query": (n((D, Q)) * 0.4 / np.sqrt(D) * fd[:, None]).astype(np.float32),
        "keys_words": keysp[0],
        "keys_scales": keysp[1],
        "gain": (np.random.uniform(0.3, 0.8, (Q, 1))).astype(np.float32),
        "os": (np.random.uniform(4.0, 16.0, (1, I)) * fi).astype(np.float32),
        "vals": (n((E, T)) / ti).astype(np.float32),
        "offs": striped(idx),
    }


def reference(query, keys_words, keys_scales, gain, os, vals, offs):
    idx = unstriped(offs)
    keysu = unpack_weight(keys_words, keys_scales, "e2m1")
    queryq = mxq(f64(query), 0, "e4m3")
    keysidxg = keysu[:, idx]
    a = queryq.T @ keysidxg
    p = np.exp(a - np.max(a, axis=1, keepdims=True))
    z = np.sum(p, axis=1, keepdims=True)
    u1 = p / z * f64(gain) * 512.0
    p2 = np.exp(u1 - np.max(u1, axis=1, keepdims=True))
    z2 = np.sum(p2, axis=1, keepdims=True)
    w = p2 / z2
    wo1 = w * f64(os)
    wt1 = wo1.T
    vt1 = f64(vals)[:, idx].T
    wt1q = mxq(wt1, 0, "e4m3")
    vt1q = mxq(vt1, 0, "e4m3")
    o = wt1q.T @ vt1q
    return o

@@ -1,0 +1,124 @@
+from contextlib import ExitStack
+
+import concourse.mybir as mybir
+from concourse.masks import make_identity
+
+D, E, T, I, Q = 512, 512, 2048, 512, 128
+FLOPS = 2 * Q * D * I + 2 * Q * I * E
+
+F32 = mybir.dt.float32
+BF16 = mybir.dt.bfloat16
+I32 = mybir.dt.int32
+U32 = mybir.dt.uint32
+U16 = mybir.dt.uint16
+U8 = mybir.dt.uint8
+FP8X4 = mybir.dt.float8_e4m3fn_x4
+FP4X4 = mybir.dt.float4_e2m1fn_x4
+ALU = mybir.AluOpType
+ACT = mybir.ActivationFunctionType
+AX = mybir.AxisListType
+
+P = 128
+PACK = 4
+TILES = E // P
+LAST_ON_VECTOR = 288
+
+
+def tile_attend_doubled_kernel(tc, query, keys_words, keys_scales, gain, slot_factor, vals, offs, out):
+    nc = tc.nc
+    with ExitStack() as ctx:
+        keep = ctx.enter_context(tc.tile_pool(name="keep", bufs=1))
+        psum = ctx.enter_context(tc.psum_pool(name="psum", bufs=1))
+
+        offsets = keep.tile([P, I // 16], U16, name="offsets")
+        key_bytes = keep.tile([P, T], U8, name="key_bytes", align_bytes=64)
+        key_words = keep.tile([P, T], U16, name="key_words", tag="shared3", align_bytes=64)
+        query_raw = keep.tile([P, PACK, Q], F32, name="query_raw", tag="shared2", align_bytes=64)
+        pools = [keep.tile([P, T], F32, name="pool%d" % j, align_bytes=64) for j in range(2)]
+        gain_col = keep.tile([P, 1], F32, name="gain_col")
+        factor = keep.tile([P, PACK], F32, name="factor")
+        ident = keep.tile([P, P], F32, name="ident")
+
+        nc.vector.memset(key_bytes[:].bitcast(I32), 0)
+        nc.sync.dma_start(offsets[:], offs)
+        for g in range(4):
+            nc.scalar.dma_start(key_bytes[32 * g : 32 * g + 4, :].bitcast(I32), keys_scales[0, 4 * g : 4 * g + 4, :].bitcast(I32))
+        nc.sync.dma_start(key_words[:].bitcast(I32), keys_words[0].bitcast(I32))
+        nc.sync.dma_start(query_raw[:], query.rearrange("(p t) q -> p t q", t=PACK))
+        for j in range(2):
+            nc.sync.dma_start(pools[j][:], vals[j * P : (j + 1) * P, :])
+        make_identity(nc, ident[:])
+        nc.gpsimd.dma_start(gain_col[:], gain)
+        nc.gpsimd.dma_start(factor[:], slot_factor.rearrange("o (p t) -> (o p) t", t=PACK))
+
+        listed_bytes = keep.tile([P, I], U8, name="listed_bytes", align_bytes=64)
+        listed_words = keep.tile([P, I], U16, name="listed_words", align_bytes=64)
+        nc.vector.tensor_copy(listed_bytes[:], key_bytes[:].indirect(offsets[:]))
+        nc.vector.tensor_copy(listed_words[:], key_words[:].indirect(offsets[:]))
+
+        query_bf = keep.tile([P, Q, PACK], BF16, name="query_bf", align_bytes=64)
+        nc.scalar.copy(query_bf[:], query_raw[:].rearrange("p t q -> p q t"))
+        for j in range(2, TILES):
+            pools.append(keep.tile([P, T], F32, name="pool%d" % j, tag="shared%d" % j, align_bytes=64))
+            nc.sync.dma_start(pools[j][:], vals[j * P : (j + 1) * P, :])
+        query_codes = keep.tile([P, Q], U32, name="query_codes", align_bytes=64)
+        query_scales = keep.tile([P, Q], U8, name="query_scales", align_bytes=64)
+        nc.vector.quantize_mx(out=query_codes[:].bitcast(FP8X4), scales=query_scales[:], in_=query_bf[:].rearrange("p q t -> p (q t)"))
+
+        scores = psum.tile([P, I], F32, name="scores")
+        nc.tensor.matmul_mx(out=scores[:], lhsT=query_codes[:].bitcast(FP8X4), lhsT_scale=query_scales[:],
+                            rhs=listed_words[:].bitcast(FP4X4), rhs_scale=listed_bytes[:], start=True, stop=True)
+
+        neg_max = keep.tile([P, 1], F32, name="neg_max")
+        nc.vector.tensor_reduce(out=neg_max[:], in_=scores[:], axis=AX.X, op=ALU.max, negate=True)
+        p1 = keep.tile([P, PACK, P], F32, name="p1")
+        z1 = keep.tile([P, 1], F32, name="z1")
+        nc.scalar.activation(out=p1[:], in_=scores[:].rearrange("q (s t) -> q t s", t=PACK), func=ACT.Exp, bias=neg_max[:], accum_out=z1[:])
+        r1 = keep.tile([P, 1], F32, name="r1")
+        nc.vector.reciprocal(r1[:], z1[:])
+        neg_c = keep.tile([P, 1], F32, name="neg_c")
+        nc.vector.tensor_scalar(out=neg_c[:], in0=r1[:], scalar1=gain_col[:], scalar2=-float(I), op0=ALU.mult, op1=ALU.mult)
+        neg_u = keep.tile([P, I], F32, name="neg_u")
+        neg_max2 = keep.tile([P, 1], F32, name="neg_max2")
+        nc.vector.tensor_scalar(out=neg_u[:], in0=p1[:].rearrange("q t s -> q (t s)"), scalar1=neg_c[:], scalar2=None,
+                                op0=ALU.mult, op1=ALU.min, accum_out=neg_max2[:])
+        p2 = keep.tile([P, I], F32, name="p2")
+        z2 = keep.tile([P, 1], F32, name="z2")
+        nc.scalar.activation(out=p2[:], in_=neg_u[:], func=ACT.Exp, bias=neg_max2[:], scale=-1.0, accum_out=z2[:])
+        r2 = keep.tile([P, 1], F32, name="r2")
+        nc.vector.reciprocal(r2[:], z2[:])
+        w = keep.tile([P, I], F32, name="w")
+        nc.vector.tensor_scalar(out=w[:], in0=p2[:], scalar1=r2[:], scalar2=None, op0=ALU.mult)
+        w_turned = psum.tile([P, PACK, Q], F32, name="w_turned")
+        for t in range(PACK):
+            nc.tensor.transpose(w_turned[:, t, :], w[:, t * P : (t + 1) * P], ident[:])
+        w_bf = keep.tile([P, Q, PACK], BF16, name="w_bf", align_bytes=64)
+        nc.vector.tensor_tensor(out=w_bf[:], in0=w_turned[:].rearrange("p t q -> p q t"),
+                                in1=factor[:].unsqueeze(1).to_broadcast([P, Q, PACK]), op=ALU.mult)
+        w_codes = keep.tile([P, Q], U32, name="w_codes", align_bytes=64)
+        w_scales = keep.tile([P, Q], U8, name="w_scales", align_bytes=64)
+        nc.vector.quantize_mx(out=w_codes[:].bitcast(FP8X4), scales=w_scales[:], in_=w_bf[:].rearrange("p q t -> p (q t)"))
+
+        result = keep.tile([P, E], F32, name="result")
+        for j in range(TILES):
+            listed = keep.tile([P, I], BF16, name="listed%d" % j, align_bytes=64)
+            cut = LAST_ON_VECTOR if j == TILES - 1 else 0
+            if cut:
+                nc.vector.tensor_copy(listed[:, :cut], pools[j][:].indirect(offsets[:, : cut // 16]))
+            nc.scalar.activation(listed[:, cut:], pools[j][:].indirect(offsets[:, cut // 16 :]), ACT.Copy)
+            pairs = listed[:].bitcast(F32)
+            turned = psum.tile([P, 2, P], F32, name="turned%d" % (j % 2))
+            for u in range(2):
+                nc.tensor.transpose(turned[:, u, :], pairs[:, u::2], ident[:])
+            v_bf = keep.tile([P, P * PACK], BF16, name="v_bf%d" % j, align_bytes=64)
+            nc.vector.tensor_copy(v_bf[:].bitcast(F32).rearrange("p (e u) -> p e u", u=2), turned[:].rearrange("p u e -> p e u"))
+            v_codes = keep.tile([P, P], U32, name="v_codes%d" % j, align_bytes=64)
+            v_scales = keep.tile([P, P], U8, name="v_scales%d" % j, align_bytes=64)
+            nc.vector.quantize_mx(out=v_codes[:].bitcast(FP8X4), scales=v_scales[:], in_=v_bf[:])
+            sums = psum.tile([P, P], F32, name="sums%d" % j)
+            nc.tensor.matmul_mx(out=sums[:], lhsT=w_codes[:].bitcast(FP8X4), lhsT_scale=w_scales[:],
+                                rhs=v_codes[:].bitcast(FP8X4), rhs_scale=v_scales[:], start=True, stop=True)
+            nc.scalar.copy(result[:, j * P : (j + 1) * P], sums[:])
+            if j == TILES - 2:
+                nc.sync.dma_start(out[:, : (j + 1) * P], result[:, : (j + 1) * P])
+        nc.sync.dma_start(out[:, E - P :], result[:, E - P :])

@@ -21,7 +21,7 @@ AX = mybir.AxisListType
 P = 128
 PACK = 4
 TILES = E // P
-LAST_ON_VECTOR = 288
+ON_VECTOR = (0, 320, 0, 288)
 
 
 def tile_attend_doubled_kernel(tc, query, keys_words, keys_scales, gain, slot_factor, vals, offs, out):
@@ -32,93 +32,133 @@ def tile_attend_doubled_kernel(tc, query, keys_words, keys_scales, gain, slot_fa
 
         offsets = keep.tile([P, I // 16], U16, name="offsets")
         key_bytes = keep.tile([P, T], U8, name="key_bytes", align_bytes=64)
-        key_words = keep.tile([P, T], U16, name="key_words", tag="shared3", align_bytes=64)
-        query_raw = keep.tile([P, PACK, Q], F32, name="query_raw", tag="shared2", align_bytes=64)
-        pools = [keep.tile([P, T], F32, name="pool%d" % j, align_bytes=64) for j in range(2)]
-        gain_col = keep.tile([P, 1], F32, name="gain_col")
-        factor = keep.tile([P, PACK], F32, name="factor")
+        key_words = keep.tile([P, T], U16, name="key_words", align_bytes=64)
+        query_raw = keep.tile([P, PACK, Q], F32, name="query_raw")
         ident = keep.tile([P, P], F32, name="ident")
+        pools = [keep.tile([P, T], F32, name="pool%d" % j, tag="pool%d" % j) for j in range(TILES)]
+        gain_col = keep.tile([P, 1], F32, name="gain_col")
+        factor = keep.tile([P, PACK], F32, name="factor", tag="listed3", align_bytes=64)
 
         nc.vector.memset(key_bytes[:].bitcast(I32), 0)
         nc.sync.dma_start(offsets[:], offs)
         for g in range(4):
-            nc.scalar.dma_start(key_bytes[32 * g : 32 * g + 4, :].bitcast(I32), keys_scales[0, 4 * g : 4 * g + 4, :].bitcast(I32))
+            nc.sync.dma_start(key_bytes[32 * g : 32 * g + 4, :].bitcast(I32), keys_scales[0, 4 * g : 4 * g + 4, :].bitcast(I32))
         nc.sync.dma_start(key_words[:].bitcast(I32), keys_words[0].bitcast(I32))
         nc.sync.dma_start(query_raw[:], query.rearrange("(p t) q -> p t q", t=PACK))
-        for j in range(2):
+        for j in range(TILES):
             nc.sync.dma_start(pools[j][:], vals[j * P : (j + 1) * P, :])
+            if j == 0:
+                nc.sync.dma_start(gain_col[:], gain)
+                nc.sync.dma_start(factor[:], slot_factor.rearrange("o (p t) -> (o p) t", t=PACK))
         make_identity(nc, ident[:])
-        nc.gpsimd.dma_start(gain_col[:], gain)
-        nc.gpsimd.dma_start(factor[:], slot_factor.rearrange("o (p t) -> (o p) t", t=PACK))
 
-        listed_bytes = keep.tile([P, I], U8, name="listed_bytes", align_bytes=64)
+        half = I // 2
         listed_words = keep.tile([P, I], U16, name="listed_words", align_bytes=64)
-        nc.vector.tensor_copy(listed_bytes[:], key_bytes[:].indirect(offsets[:]))
         nc.vector.tensor_copy(listed_words[:], key_words[:].indirect(offsets[:]))
 
-        query_bf = keep.tile([P, Q, PACK], BF16, name="query_bf", align_bytes=64)
+        query_bf = keep.tile([P, Q, PACK], BF16, name="query_bf", tag="query_bf", align_bytes=64)
         nc.scalar.copy(query_bf[:], query_raw[:].rearrange("p t q -> p q t"))
-        for j in range(2, TILES):
-            pools.append(keep.tile([P, T], F32, name="pool%d" % j, tag="shared%d" % j, align_bytes=64))
-            nc.sync.dma_start(pools[j][:], vals[j * P : (j + 1) * P, :])
         query_codes = keep.tile([P, Q], U32, name="query_codes", align_bytes=64)
         query_scales = keep.tile([P, Q], U8, name="query_scales", align_bytes=64)
         nc.vector.quantize_mx(out=query_codes[:].bitcast(FP8X4), scales=query_scales[:], in_=query_bf[:].rearrange("p q t -> p (q t)"))
 
-        scores = psum.tile([P, I], F32, name="scores")
-        nc.tensor.matmul_mx(out=scores[:], lhsT=query_codes[:].bitcast(FP8X4), lhsT_scale=query_scales[:],
-                            rhs=listed_words[:].bitcast(FP4X4), rhs_scale=listed_bytes[:], start=True, stop=True)
+        scores = []
+        for h in range(2):
+            cols = slice(h * half, (h + 1) * half)
+            listed_bytes = keep.tile([P, half], U8, name="listed_bytes%d" % h, tag="query_bf" if h else "listed_bytes0", align_bytes=64)
+            nc.vector.tensor_copy(listed_bytes[:], key_bytes[:].indirect(offsets[:, h * half // 16 : (h + 1) * half // 16]))
+            scores.append(psum.tile([P, half], F32, name="scores%d" % h, tag="turned%d" % (2 - 2 * h)))
+            nc.tensor.matmul_mx(out=scores[h][:], lhsT=query_codes[:].bitcast(FP8X4), lhsT_scale=query_scales[:],
+                                rhs=listed_words[:, cols].bitcast(FP4X4), rhs_scale=listed_bytes[:], start=True, stop=True)
 
+        def gather_values(j):
+            listed = keep.tile([P, I], BF16, name="listed%d" % j, tag="listed%d" % j, align_bytes=64)
+            cut = ON_VECTOR[j]
+            if cut:
+                nc.vector.tensor_copy(listed[:, :cut], pools[j][:].indirect(offsets[:, : cut // 16]))
+            nc.scalar.activation(listed[:, cut:], pools[j][:].indirect(offsets[:, cut // 16 :]), ACT.Copy)
+            return listed
+
+        def turn_values(j, listed):
+            pairs = listed[:].bitcast(F32)
+            turned = psum.tile([P, 2, P], F32, name="turned%d" % j, tag="turned%d" % j)
+            for u in range(2):
+                nc.tensor.transpose(turned[:, u, :], pairs[:, u::2], ident[:])
+            v_bf = keep.tile([P, P * PACK], BF16, name="v_bf%d" % j, tag="v_bf%d" % j, align_bytes=64)
+            move = nc.scalar.copy if j >= 2 else nc.vector.tensor_copy
+            move(v_bf[:].bitcast(F32).rearrange("p (e u) -> p e u", u=2), turned[:].rearrange("p u e -> p e u"))
+            return v_bf
+
+        listed0 = gather_values(0)
+
+        neg_a = keep.tile([P, PACK, P], F32, name="neg_a")
+        neg_max_half = keep.tile([P, 1], F32, name="neg_max_half")
         neg_max = keep.tile([P, 1], F32, name="neg_max")
-        nc.vector.tensor_reduce(out=neg_max[:], in_=scores[:], axis=AX.X, op=ALU.max, negate=True)
-        p1 = keep.tile([P, PACK, P], F32, name="p1")
+        for h in range(2):
+            nc.vector.tensor_scalar(out=neg_a[:, :, h * P // 2 : (h + 1) * P // 2], in0=scores[h][:].rearrange("q (s t) -> q t s", t=PACK),
+                                    scalar1=-1.0, scalar2=neg_max_half[:] if h else None,
+                                    op0=ALU.mult, op1=ALU.min, accum_out=(neg_max if h else neg_max_half)[:])
+        neg_flat = neg_a[:].rearrange("q t s -> q (t s)")
+        p1 = keep.tile([P, I], F32, name="p1", tag="pool0")
         z1 = keep.tile([P, 1], F32, name="z1")
-        nc.scalar.activation(out=p1[:], in_=scores[:].rearrange("q (s t) -> q t s", t=PACK), func=ACT.Exp, bias=neg_max[:], accum_out=z1[:])
-        r1 = keep.tile([P, 1], F32, name="r1")
+        nc.scalar.activation(out=p1[:], in_=neg_flat, func=ACT.Exp, bias=neg_max[:], scale=-1.0, accum_out=z1[:])
+        neg_min = keep.tile([P, 1], F32, name="neg_min")
+        nc.vector.tensor_reduce(out=neg_min[:], in_=neg_flat, axis=AX.X, op=ALU.max)
+        p_min = keep.tile([P, 1], F32, name="p_min")
+        nc.scalar.activation(out=p_min[:], in_=neg_min[:], func=ACT.Exp, bias=neg_max[:], scale=-1.0)
+        v_bf0 = turn_values(0, listed0)
+
+        r1 = keep.tile([P, 1], F32, name="r1", tag="listed1", align_bytes=64)
         nc.vector.reciprocal(r1[:], z1[:])
-        neg_c = keep.tile([P, 1], F32, name="neg_c")
-        nc.vector.tensor_scalar(out=neg_c[:], in0=r1[:], scalar1=gain_col[:], scalar2=-float(I), op0=ALU.mult, op1=ALU.mult)
-        neg_u = keep.tile([P, I], F32, name="neg_u")
+        top = keep.tile([P, 1], F32, name="top", tag="codes01", align_bytes=64)
+        nc.vector.tensor_scalar(out=top[:], in0=p_min[:], scalar1=gain_col[:], scalar2=gain_col[:], op0=ALU.mult, op1=ALU.max)
+        slope = keep.tile([P, 1], F32, name="slope", tag="listed2", align_bytes=64)
+        nc.vector.tensor_scalar(out=slope[:], in0=gain_col[:], scalar1=float(I), scalar2=r1[:], op0=ALU.mult, op1=ALU.mult)
         neg_max2 = keep.tile([P, 1], F32, name="neg_max2")
-        nc.vector.tensor_scalar(out=neg_u[:], in0=p1[:].rearrange("q t s -> q (t s)"), scalar1=neg_c[:], scalar2=None,
-                                op0=ALU.mult, op1=ALU.min, accum_out=neg_max2[:])
+        nc.vector.tensor_scalar(out=neg_max2[:], in0=top[:], scalar1=-float(I), scalar2=r1[:], op0=ALU.mult, op1=ALU.mult)
         p2 = keep.tile([P, I], F32, name="p2")
         z2 = keep.tile([P, 1], F32, name="z2")
-        nc.scalar.activation(out=p2[:], in_=neg_u[:], func=ACT.Exp, bias=neg_max2[:], scale=-1.0, accum_out=z2[:])
-        r2 = keep.tile([P, 1], F32, name="r2")
+        nc.scalar.activation(out=p2[:], in_=p1[:], func=ACT.Exp, bias=neg_max2[:], scale=slope[:], accum_out=z2[:])
+
+        codes01 = keep.tile([P, 2 * P], U32, name="codes01", tag="codes01", align_bytes=64)
+        scales01 = keep.tile([P, 2 * P], U8, name="scales01", align_bytes=64)
+        nc.vector.quantize_mx(out=codes01[:, :P].bitcast(FP8X4), scales=scales01[:, :P], in_=v_bf0[:])
+        listed1 = gather_values(1)
+
+        r2 = keep.tile([P, 1], F32, name="r2", tag="v_bf1", align_bytes=64)
         nc.vector.reciprocal(r2[:], z2[:])
         w = keep.tile([P, I], F32, name="w")
         nc.vector.tensor_scalar(out=w[:], in0=p2[:], scalar1=r2[:], scalar2=None, op0=ALU.mult)
+        v_bf1 = turn_values(1, listed1)
         w_turned = psum.tile([P, PACK, Q], F32, name="w_turned")
         for t in range(PACK):
             nc.tensor.transpose(w_turned[:, t, :], w[:, t * P : (t + 1) * P], ident[:])
-        w_bf = keep.tile([P, Q, PACK], BF16, name="w_bf", align_bytes=64)
+        nc.vector.quantize_mx(out=codes01[:, P:].bitcast(FP8X4), scales=scales01[:, P:], in_=v_bf1[:])
+        v_bf2 = turn_values(2, gather_values(2))
+        w_bf = keep.tile([P, Q, PACK], BF16, name="w_bf", tag="codes2", align_bytes=64)
         nc.vector.tensor_tensor(out=w_bf[:], in0=w_turned[:].rearrange("p t q -> p q t"),
                                 in1=factor[:].unsqueeze(1).to_broadcast([P, Q, PACK]), op=ALU.mult)
         w_codes = keep.tile([P, Q], U32, name="w_codes", align_bytes=64)
         w_scales = keep.tile([P, Q], U8, name="w_scales", align_bytes=64)
         nc.vector.quantize_mx(out=w_codes[:].bitcast(FP8X4), scales=w_scales[:], in_=w_bf[:].rearrange("p q t -> p (q t)"))
+        listed3 = gather_values(3)
+        codes2 = keep.tile([P, P], U32, name="codes2", tag="codes2", align_bytes=64)
+        scales2 = keep.tile([P, P], U8, name="scales2", align_bytes=64)
+        nc.vector.quantize_mx(out=codes2[:].bitcast(FP8X4), scales=scales2[:], in_=v_bf2[:])
+        v_bf3 = turn_values(3, listed3)
+        codes3 = keep.tile([P, P], U32, name="codes3", align_bytes=64)
+        scales3 = keep.tile([P, P], U8, name="scales3", align_bytes=64)
+        nc.vector.quantize_mx(out=codes3[:].bitcast(FP8X4), scales=scales3[:], in_=v_bf3[:])
 
-        result = keep.tile([P, E], F32, name="result")
-        for j in range(TILES):
-            listed = keep.tile([P, I], BF16, name="listed%d" % j, align_bytes=64)
-            cut = LAST_ON_VECTOR if j == TILES - 1 else 0
-            if cut:
-                nc.vector.tensor_copy(listed[:, :cut], pools[j][:].indirect(offsets[:, : cut // 16]))
-            nc.scalar.activation(listed[:, cut:], pools[j][:].indirect(offsets[:, cut // 16 :]), ACT.Copy)
-            pairs = listed[:].bitcast(F32)
-            turned = psum.tile([P, 2, P], F32, name="turned%d" % (j % 2))
-            for u in range(2):
-                nc.tensor.transpose(turned[:, u, :], pairs[:, u::2], ident[:])
-            v_bf = keep.tile([P, P * PACK], BF16, name="v_bf%d" % j, align_bytes=64)
-            nc.vector.tensor_copy(v_bf[:].bitcast(F32).rearrange("p (e u) -> p e u", u=2), turned[:].rearrange("p u e -> p e u"))
-            v_codes = keep.tile([P, P], U32, name="v_codes%d" % j, align_bytes=64)
-            v_scales = keep.tile([P, P], U8, name="v_scales%d" % j, align_bytes=64)
-            nc.vector.quantize_mx(out=v_codes[:].bitcast(FP8X4), scales=v_scales[:], in_=v_bf[:])
-            sums = psum.tile([P, P], F32, name="sums%d" % j)
+        result = keep.tile([P, E], F32, name="result", tag="pool3")
+        start = 0
+        for k, (codes, scales) in enumerate(((codes01, scales01), (codes2, scales2), (codes3, scales3))):
+            width = codes.shape[1]
+            sums = psum.tile([P, width], F32, name="sums%d" % k)
             nc.tensor.matmul_mx(out=sums[:], lhsT=w_codes[:].bitcast(FP8X4), lhsT_scale=w_scales[:],
-                                rhs=v_codes[:].bitcast(FP8X4), rhs_scale=v_scales[:], start=True, stop=True)
-            nc.scalar.copy(result[:, j * P : (j + 1) * P], sums[:])
-            if j == TILES - 2:
-                nc.sync.dma_start(out[:, : (j + 1) * P], result[:, : (j + 1) * P])
-        nc.sync.dma_start(out[:, E - P :], result[:, E - P :])
+                                rhs=codes[:].bitcast(FP8X4), rhs_scale=scales[:], start=True, stop=True)
+            nc.scalar.copy(result[:, start : start + width], sums[:])
+            start = start + width
+            if k == 1:
+                nc.sync.dma_start(out[:, :start], result[:, :start])
+        nc.scalar.dma_start(out[:, E - P :], result[:, E - P :])

@@ -21,7 +21,8 @@ AX = mybir.AxisListType
 P = 128
 PACK = 4
 TILES = E // P
-ON_VECTOR = (0, 320, 0, 288)
+FIRST_ON_VECTOR = 256
+LAST_ON_VECTOR = 288
 
 
 def tile_attend_doubled_kernel(tc, query, keys_words, keys_scales, gain, slot_factor, vals, offs, out):
@@ -35,15 +36,15 @@ def tile_attend_doubled_kernel(tc, query, keys_words, keys_scales, gain, slot_fa
         key_words = keep.tile([P, T], U16, name="key_words", align_bytes=64)
         query_raw = keep.tile([P, PACK, Q], F32, name="query_raw")
         ident = keep.tile([P, P], F32, name="ident")
-        pools = [keep.tile([P, T], F32, name="pool%d" % j, tag="pool%d" % j) for j in range(TILES)]
+        pools = [keep.tile([P, T], F32, name="pool%d" % j, tag="pool%d" % j, align_bytes=64) for j in range(TILES)]
         gain_col = keep.tile([P, 1], F32, name="gain_col")
-        factor = keep.tile([P, PACK], F32, name="factor", tag="listed3", align_bytes=64)
+        factor = keep.tile([P, PACK], F32, name="factor")
 
         nc.vector.memset(key_bytes[:].bitcast(I32), 0)
+        nc.sync.dma_start(key_words[:].bitcast(I32), keys_words[0].bitcast(I32))
         nc.sync.dma_start(offsets[:], offs)
         for g in range(4):
             nc.sync.dma_start(key_bytes[32 * g : 32 * g + 4, :].bitcast(I32), keys_scales[0, 4 * g : 4 * g + 4, :].bitcast(I32))
-        nc.sync.dma_start(key_words[:].bitcast(I32), keys_words[0].bitcast(I32))
         nc.sync.dma_start(query_raw[:], query.rearrange("(p t) q -> p t q", t=PACK))
         for j in range(TILES):
             nc.sync.dma_start(pools[j][:], vals[j * P : (j + 1) * P, :])
@@ -67,98 +68,117 @@ def tile_attend_doubled_kernel(tc, query, keys_words, keys_scales, gain, slot_fa
             cols = slice(h * half, (h + 1) * half)
             listed_bytes = keep.tile([P, half], U8, name="listed_bytes%d" % h, tag="query_bf" if h else "listed_bytes0", align_bytes=64)
             nc.vector.tensor_copy(listed_bytes[:], key_bytes[:].indirect(offsets[:, h * half // 16 : (h + 1) * half // 16]))
-            scores.append(psum.tile([P, half], F32, name="scores%d" % h, tag="turned%d" % (2 - 2 * h)))
+            scores.append(psum.tile([P, half], F32, name="scores%d" % h, tag="bank%d" % h))
             nc.tensor.matmul_mx(out=scores[h][:], lhsT=query_codes[:].bitcast(FP8X4), lhsT_scale=query_scales[:],
                                 rhs=listed_words[:, cols].bitcast(FP4X4), rhs_scale=listed_bytes[:], start=True, stop=True)
 
-        def gather_values(j):
-            listed = keep.tile([P, I], BF16, name="listed%d" % j, tag="listed%d" % j, align_bytes=64)
-            cut = ON_VECTOR[j]
-            if cut:
-                nc.vector.tensor_copy(listed[:, :cut], pools[j][:].indirect(offsets[:, : cut // 16]))
-            nc.scalar.activation(listed[:, cut:], pools[j][:].indirect(offsets[:, cut // 16 :]), ACT.Copy)
-            return listed
-
-        def turn_values(j, listed):
-            pairs = listed[:].bitcast(F32)
-            turned = psum.tile([P, 2, P], F32, name="turned%d" % j, tag="turned%d" % j)
+        def turn_pairs(pairs, bank):
+            turned = psum.tile([P, 2, P], F32, name="turned_" + bank, tag=bank)
             for u in range(2):
-                nc.tensor.transpose(turned[:, u, :], pairs[:, u::2], ident[:])
-            v_bf = keep.tile([P, P * PACK], BF16, name="v_bf%d" % j, tag="v_bf%d" % j, align_bytes=64)
-            move = nc.scalar.copy if j >= 2 else nc.vector.tensor_copy
-            move(v_bf[:].bitcast(F32).rearrange("p (e u) -> p e u", u=2), turned[:].rearrange("p u e -> p e u"))
-            return v_bf
+                nc.tensor.transpose(turned[:, u, :], pairs[u], ident[:])
+            return turned
 
-        listed0 = gather_values(0)
+        def turn_values(listed, bank):
+            words = listed[:].bitcast(F32)
+            return turn_pairs([words[:, u::2] for u in range(2)], bank)
 
-        neg_a = keep.tile([P, PACK, P], F32, name="neg_a")
+        def interleave(move, grouped, turned):
+            move(grouped.bitcast(F32).rearrange("p (c u) -> p c u", u=2), turned[:].rearrange("p u c -> p c u"))
+
+        def quantise(name, grouped, tag):
+            width = grouped.shape[1] // PACK
+            codes = keep.tile([P, width], U32, name=name + "_codes", tag=tag, align_bytes=64)
+            scales = keep.tile([P, width], U8, name=name + "_scales", align_bytes=64)
+            nc.vector.quantize_mx(out=codes[:].bitcast(FP8X4), scales=scales[:], in_=grouped)
+            return codes, scales
+
+        listed0 = keep.tile([P, I], BF16, name="listed0", align_bytes=64)
+
+        neg_a = keep.tile([P, 2, half], F32, name="neg_a")
         neg_max_half = keep.tile([P, 1], F32, name="neg_max_half")
         neg_max = keep.tile([P, 1], F32, name="neg_max")
         for h in range(2):
-            nc.vector.tensor_scalar(out=neg_a[:, :, h * P // 2 : (h + 1) * P // 2], in0=scores[h][:].rearrange("q (s t) -> q t s", t=PACK),
+            nc.vector.tensor_scalar(out=neg_a[:, :, h * P : (h + 1) * P].rearrange("q u (s e) -> q u s e", e=2),
+                                    in0=scores[h][:].rearrange("q (s u e) -> q u s e", u=2, e=2),
                                     scalar1=-1.0, scalar2=neg_max_half[:] if h else None,
                                     op0=ALU.mult, op1=ALU.min, accum_out=(neg_max if h else neg_max_half)[:])
-        neg_flat = neg_a[:].rearrange("q t s -> q (t s)")
-        p1 = keep.tile([P, I], F32, name="p1", tag="pool0")
+        neg_flat = neg_a[:].rearrange("q u c -> q (u c)")
+        p1 = keep.tile([P, I], F32, name="p1")
         z1 = keep.tile([P, 1], F32, name="z1")
         nc.scalar.activation(out=p1[:], in_=neg_flat, func=ACT.Exp, bias=neg_max[:], scale=-1.0, accum_out=z1[:])
         neg_min = keep.tile([P, 1], F32, name="neg_min")
         nc.vector.tensor_reduce(out=neg_min[:], in_=neg_flat, axis=AX.X, op=ALU.max)
         p_min = keep.tile([P, 1], F32, name="p_min")
         nc.scalar.activation(out=p_min[:], in_=neg_min[:], func=ACT.Exp, bias=neg_max[:], scale=-1.0)
-        v_bf0 = turn_values(0, listed0)
 
-        r1 = keep.tile([P, 1], F32, name="r1", tag="listed1", align_bytes=64)
-        nc.vector.reciprocal(r1[:], z1[:])
-        top = keep.tile([P, 1], F32, name="top", tag="codes01", align_bytes=64)
+        nc.scalar.activation(listed0[:, FIRST_ON_VECTOR:], pools[0][:].indirect(offsets[:, FIRST_ON_VECTOR // 16 :]), ACT.Copy)
+        factor_rows = psum.tile([P, 2, P, 2], F32, name="factor_rows", tag="bank1")
+        for t in range(PACK):
+            nc.tensor.transpose(factor_rows[:, t // 2, :, t % 2], factor[:, t : t + 1].to_broadcast([P, P]), ident[:])
+
+        r1 = listed0[:].bitcast(F32)[:, 0:1]
+        nc.vector.reciprocal(r1, z1[:])
+        top = keep.tile([P, 1], F32, name="top")
         nc.vector.tensor_scalar(out=top[:], in0=p_min[:], scalar1=gain_col[:], scalar2=gain_col[:], op0=ALU.mult, op1=ALU.max)
-        slope = keep.tile([P, 1], F32, name="slope", tag="listed2", align_bytes=64)
-        nc.vector.tensor_scalar(out=slope[:], in0=gain_col[:], scalar1=float(I), scalar2=r1[:], op0=ALU.mult, op1=ALU.mult)
-        neg_max2 = keep.tile([P, 1], F32, name="neg_max2")
-        nc.vector.tensor_scalar(out=neg_max2[:], in0=top[:], scalar1=-float(I), scalar2=r1[:], op0=ALU.mult, op1=ALU.mult)
-        p2 = keep.tile([P, I], F32, name="p2")
+        slope = keep.tile([P, 1], F32, name="slope")
+        nc.vector.tensor_scalar(out=slope[:], in0=gain_col[:], scalar1=float(I), scalar2=r1, op0=ALU.mult, op1=ALU.mult)
+        neg_max2 = keep.tile([P, 1], F32, name="neg_max2", tag="listed1", align_bytes=64)
+        nc.vector.tensor_scalar(out=neg_max2[:], in0=top[:], scalar1=-float(I), scalar2=r1, op0=ALU.mult, op1=ALU.mult)
+        p2 = keep.tile([P, I], F32, name="p2", tag="grouped_w0", align_bytes=64)
         z2 = keep.tile([P, 1], F32, name="z2")
         nc.scalar.activation(out=p2[:], in_=p1[:], func=ACT.Exp, bias=neg_max2[:], scale=slope[:], accum_out=z2[:])
+        nc.vector.tensor_copy(listed0[:, :FIRST_ON_VECTOR], pools[0][:].indirect(offsets[:, : FIRST_ON_VECTOR // 16]))
+        turned0 = turn_values(listed0, "bank0")
+        listed1 = keep.tile([P, I], BF16, name="listed1", tag="listed1", align_bytes=64)
+        nc.scalar.activation(listed1[:], pools[1][:].indirect(offsets[:]), ACT.Copy)
+        listed2 = keep.tile([P, I], BF16, name="listed2", align_bytes=64)
+        nc.scalar.activation(listed2[:], pools[2][:].indirect(offsets[:]), ACT.Copy)
 
-        codes01 = keep.tile([P, 2 * P], U32, name="codes01", tag="codes01", align_bytes=64)
-        scales01 = keep.tile([P, 2 * P], U8, name="scales01", align_bytes=64)
-        nc.vector.quantize_mx(out=codes01[:, :P].bitcast(FP8X4), scales=scales01[:, :P], in_=v_bf0[:])
-        listed1 = gather_values(1)
-
-        r2 = keep.tile([P, 1], F32, name="r2", tag="v_bf1", align_bytes=64)
+        r2 = keep.tile([P, 1], F32, name="r2")
         nc.vector.reciprocal(r2[:], z2[:])
-        w = keep.tile([P, I], F32, name="w")
-        nc.vector.tensor_scalar(out=w[:], in0=p2[:], scalar1=r2[:], scalar2=None, op0=ALU.mult)
-        v_bf1 = turn_values(1, listed1)
-        w_turned = psum.tile([P, PACK, Q], F32, name="w_turned")
-        for t in range(PACK):
-            nc.tensor.transpose(w_turned[:, t, :], w[:, t * P : (t + 1) * P], ident[:])
-        nc.vector.quantize_mx(out=codes01[:, P:].bitcast(FP8X4), scales=scales01[:, P:], in_=v_bf1[:])
-        v_bf2 = turn_values(2, gather_values(2))
-        w_bf = keep.tile([P, Q, PACK], BF16, name="w_bf", tag="codes2", align_bytes=64)
-        nc.vector.tensor_tensor(out=w_bf[:], in0=w_turned[:].rearrange("p t q -> p q t"),
-                                in1=factor[:].unsqueeze(1).to_broadcast([P, Q, PACK]), op=ALU.mult)
-        w_codes = keep.tile([P, Q], U32, name="w_codes", align_bytes=64)
-        w_scales = keep.tile([P, Q], U8, name="w_scales", align_bytes=64)
-        nc.vector.quantize_mx(out=w_codes[:].bitcast(FP8X4), scales=w_scales[:], in_=w_bf[:].rearrange("p q t -> p (q t)"))
-        listed3 = gather_values(3)
-        codes2 = keep.tile([P, P], U32, name="codes2", tag="codes2", align_bytes=64)
-        scales2 = keep.tile([P, P], U8, name="scales2", align_bytes=64)
-        nc.vector.quantize_mx(out=codes2[:].bitcast(FP8X4), scales=scales2[:], in_=v_bf2[:])
-        v_bf3 = turn_values(3, listed3)
-        codes3 = keep.tile([P, P], U32, name="codes3", align_bytes=64)
-        scales3 = keep.tile([P, P], U8, name="scales3", align_bytes=64)
-        nc.vector.quantize_mx(out=codes3[:].bitcast(FP8X4), scales=scales3[:], in_=v_bf3[:])
+        w_bf = keep.tile([P, I], BF16, name="w_bf", align_bytes=64)
+        nc.vector.scalar_tensor_tensor(out=w_bf[:], in0=p2[:], scalar=r2[:], in1=factor_rows[:].rearrange("q u s e -> q (u s e)"),
+                                       op0=ALU.mult, op1=ALU.mult)
+        w_words = w_bf[:].bitcast(F32)
+        w_turned = turn_pairs([w_words[:, u * P : (u + 1) * P] for u in range(2)], "bank2")
+        turned1 = turn_values(listed1, "bank5")
+        grouped_w0 = keep.tile([P, 2 * I], BF16, name="grouped_w0", tag="grouped_w0", align_bytes=64)
+        interleave(nc.vector.tensor_copy, grouped_w0[:, I:], turned0)
+        interleave(nc.vector.tensor_copy, grouped_w0[:, :I], w_turned)
+        codes_w0, scales_w0 = quantise("w0", grouped_w0[:], "codes_w0")
+        grouped1 = keep.tile([P, I], BF16, name="grouped1", align_bytes=64)
+        interleave(nc.vector.tensor_copy, grouped1[:], turned1)
+        values1 = quantise("values1", grouped1[:], "codes1")
+        turned2 = turn_values(listed2, "bank3")
 
-        result = keep.tile([P, E], F32, name="result", tag="pool3")
-        start = 0
-        for k, (codes, scales) in enumerate(((codes01, scales01), (codes2, scales2), (codes3, scales3))):
-            width = codes.shape[1]
-            sums = psum.tile([P, width], F32, name="sums%d" % k)
-            nc.tensor.matmul_mx(out=sums[:], lhsT=w_codes[:].bitcast(FP8X4), lhsT_scale=w_scales[:],
-                                rhs=codes[:].bitcast(FP8X4), rhs_scale=scales[:], start=True, stop=True)
-            nc.scalar.copy(result[:, start : start + width], sums[:])
-            start = start + width
-            if k == 1:
-                nc.sync.dma_start(out[:, :start], result[:, :start])
-        nc.scalar.dma_start(out[:, E - P :], result[:, E - P :])
+        listed3 = keep.tile([P, I], BF16, name="listed3", align_bytes=64)
+        nc.vector.tensor_copy(listed3[:, :LAST_ON_VECTOR], pools[3][:].indirect(offsets[:, : LAST_ON_VECTOR // 16]))
+        nc.scalar.activation(listed3[:, LAST_ON_VECTOR:], pools[3][:].indirect(offsets[:, LAST_ON_VECTOR // 16 :]), ACT.Copy)
+        turned3 = turn_values(listed3, "bank4")
+        late = keep.tile([P, 2 * half], F32, name="late", tag="pool3", align_bytes=64)
+        grouped2 = late[:, half:].bitcast(BF16)
+        interleave(nc.scalar.copy, grouped2, turned2)
+        values2 = quantise("values2", grouped2, "codes2")
+        grouped3 = keep.tile([P, I], BF16, name="grouped3", align_bytes=64)
+        interleave(nc.scalar.copy, grouped3[:], turned3)
+        values3 = quantise("values3", grouped3[:], "codes3")
+
+        def product(sums, codes, scales):
+            nc.tensor.matmul_mx(out=sums, lhsT=codes_w0[:, :P].bitcast(FP8X4), lhsT_scale=scales_w0[:, :P],
+                                rhs=codes.bitcast(FP8X4), rhs_scale=scales, start=True, stop=True)
+
+        sums01 = psum.tile([P, 2 * P], F32, name="sums01")
+        product(sums01[:, :P], codes_w0[:, P:], scales_w0[:, P:])
+        product(sums01[:, P:], values1[0][:], values1[1][:])
+        nc.vector.tensor_copy(late[:, :half], sums01[:])
+        nc.sync.dma_start(out[:, : 2 * P], late[:, :half])
+        sums2 = psum.tile([P, P], F32, name="sums2", tag="bank0")
+        product(sums2[:], values2[0][:], values2[1][:])
+        result2 = keep.tile([P, P], F32, name="result2")
+        nc.vector.tensor_copy(result2[:], sums2[:])
+        nc.sync.dma_start(out[:, 2 * P : 3 * P], result2[:])
+        sums3 = psum.tile([P, P], F32, name="sums3")
+        product(sums3[:], values3[0][:], values3[1][:])
+        result3 = keep.tile([P, P], F32, name="result3")
+        nc.scalar.copy(result3[:], sums3[:])
+        nc.scalar.dma_start(out[:, 3 * P :], result3[:])

from contextlib import ExitStack

import concourse.mybir as mybir
from concourse.masks import make_identity

D, E, T, I, Q = 512, 512, 2048, 512, 128
FLOPS = 2 * Q * D * I + 2 * Q * I * E

F32 = mybir.dt.float32
BF16 = mybir.dt.bfloat16
I32 = mybir.dt.int32
U32 = mybir.dt.uint32
U16 = mybir.dt.uint16
U8 = mybir.dt.uint8
FP8X4 = mybir.dt.float8_e4m3fn_x4
FP4X4 = mybir.dt.float4_e2m1fn_x4
ALU = mybir.AluOpType
ACT = mybir.ActivationFunctionType
AX = mybir.AxisListType

P = 128
PACK = 4
TILES = E // P
FIRST_ON_VECTOR = 256
LAST_ON_VECTOR = 288


def tile_attend_doubled_kernel(tc, query, keys_words, keys_scales, gain, slot_factor, vals, offs, out):
    nc = tc.nc
    with ExitStack() as ctx:
        keep = ctx.enter_context(tc.tile_pool(name="keep", bufs=1))
        psum = ctx.enter_context(tc.psum_pool(name="psum", bufs=1))

        offsets = keep.tile([P, I // 16], U16, name="offsets")
        key_bytes = keep.tile([P, T], U8, name="key_bytes", align_bytes=64)
        key_words = keep.tile([P, T], U16, name="key_words", align_bytes=64)
        query_raw = keep.tile([P, PACK, Q], F32, name="query_raw")
        ident = keep.tile([P, P], F32, name="ident")
        pools = [keep.tile([P, T], F32, name="pool%d" % j, tag="pool%d" % j, align_bytes=64) for j in range(TILES)]
        gain_col = keep.tile([P, 1], F32, name="gain_col")
        factor = keep.tile([P, PACK], F32, name="factor")

        nc.vector.memset(key_bytes[:].bitcast(I32), 0)
        nc.sync.dma_start(key_words[:].bitcast(I32), keys_words[0].bitcast(I32))
        nc.sync.dma_start(offsets[:], offs)
        for g in range(4):
            nc.sync.dma_start(key_bytes[32 * g : 32 * g + 4, :].bitcast(I32), keys_scales[0, 4 * g : 4 * g + 4, :].bitcast(I32))
        nc.sync.dma_start(query_raw[:], query.rearrange("(p t) q -> p t q", t=PACK))
        for j in range(TILES):
            nc.sync.dma_start(pools[j][:], vals[j * P : (j + 1) * P, :])
            if j == 0:
                nc.sync.dma_start(gain_col[:], gain)
                nc.sync.dma_start(factor[:], slot_factor.rearrange("o (p t) -> (o p) t", t=PACK))
        make_identity(nc, ident[:])

        half = I // 2
        listed_words = keep.tile([P, I], U16, name="listed_words", align_bytes=64)
        nc.vector.tensor_copy(listed_words[:], key_words[:].indirect(offsets[:]))

        query_bf = keep.tile([P, Q, PACK], BF16, name="query_bf", tag="query_bf", align_bytes=64)
        nc.scalar.copy(query_bf[:], query_raw[:].rearrange("p t q -> p q t"))
        query_codes = keep.tile([P, Q], U32, name="query_codes", align_bytes=64)
        query_scales = keep.tile([P, Q], U8, name="query_scales", align_bytes=64)
        nc.vector.quantize_mx(out=query_codes[:].bitcast(FP8X4), scales=query_scales[:], in_=query_bf[:].rearrange("p q t -> p (q t)"))

        scores = []
        for h in range(2):
            cols = slice(h * half, (h + 1) * half)
            listed_bytes = keep.tile([P, half], U8, name="listed_bytes%d" % h, tag="query_bf" if h else "listed_bytes0", align_bytes=64)
            nc.vector.tensor_copy(listed_bytes[:], key_bytes[:].indirect(offsets[:, h * half // 16 : (h + 1) * half // 16]))
            scores.append(psum.tile([P, half], F32, name="scores%d" % h, tag="bank%d" % h))
            nc.tensor.matmul_mx(out=scores[h][:], lhsT=query_codes[:].bitcast(FP8X4), lhsT_scale=query_scales[:],
                                rhs=listed_words[:, cols].bitcast(FP4X4), rhs_scale=listed_bytes[:], start=True, stop=True)

        def turn_pairs(pairs, bank):
            turned = psum.tile([P, 2, P], F32, name="turned_" + bank, tag=bank)
            for u in range(2):
                nc.tensor.transpose(turned[:, u, :], pairs[u], ident[:])
            return turned

        def turn_values(listed, bank):
            words = listed[:].bitcast(F32)
            return turn_pairs([words[:, u::2] for u in range(2)], bank)

        def interleave(move, grouped, turned):
            move(grouped.bitcast(F32).rearrange("p (c u) -> p c u", u=2), turned[:].rearrange("p u c -> p c u"))

        def quantise(name, grouped, tag):
            width = grouped.shape[1] // PACK
            codes = keep.tile([P, width], U32, name=name + "_codes", tag=tag, align_bytes=64)
            scales = keep.tile([P, width], U8, name=name + "_scales", align_bytes=64)
            nc.vector.quantize_mx(out=codes[:].bitcast(FP8X4), scales=scales[:], in_=grouped)
            return codes, scales

        listed0 = keep.tile([P, I], BF16, name="listed0", align_bytes=64)

        neg_a = keep.tile([P, 2, half], F32, name="neg_a")
        neg_max_half = keep.tile([P, 1], F32, name="neg_max_half")
        neg_max = keep.tile([P, 1], F32, name="neg_max")
        for h in range(2):
            nc.vector.tensor_scalar(out=neg_a[:, :, h * P : (h + 1) * P].rearrange("q u (s e) -> q u s e", e=2),
                                    in0=scores[h][:].rearrange("q (s u e) -> q u s e", u=2, e=2),
                                    scalar1=-1.0, scalar2=neg_max_half[:] if h else None,
                                    op0=ALU.mult, op1=ALU.min, accum_out=(neg_max if h else neg_max_half)[:])
        neg_flat = neg_a[:].rearrange("q u c -> q (u c)")
        p1 = keep.tile([P, I], F32, name="p1")
        z1 = keep.tile([P, 1], F32, name="z1")
        nc.scalar.activation(out=p1[:], in_=neg_flat, func=ACT.Exp, bias=neg_max[:], scale=-1.0, accum_out=z1[:])
        neg_min = keep.tile([P, 1], F32, name="neg_min")
        nc.vector.tensor_reduce(out=neg_min[:], in_=neg_flat, axis=AX.X, op=ALU.max)
        p_min = keep.tile([P, 1], F32, name="p_min")
        nc.scalar.activation(out=p_min[:], in_=neg_min[:], func=ACT.Exp, bias=neg_max[:], scale=-1.0)

        nc.scalar.activation(listed0[:, FIRST_ON_VECTOR:], pools[0][:].indirect(offsets[:, FIRST_ON_VECTOR // 16 :]), ACT.Copy)
        factor_rows = psum.tile([P, 2, P, 2], F32, name="factor_rows", tag="bank1")
        for t in range(PACK):
            nc.tensor.transpose(factor_rows[:, t // 2, :, t % 2], factor[:, t : t + 1].to_broadcast([P, P]), ident[:])

        r1 = listed0[:].bitcast(F32)[:, 0:1]
        nc.vector.reciprocal(r1, z1[:])
        top = keep.tile([P, 1], F32, name="top")
        nc.vector.tensor_scalar(out=top[:], in0=p_min[:], scalar1=gain_col[:], scalar2=gain_col[:], op0=ALU.mult, op1=ALU.max)
        slope = keep.tile([P, 1], F32, name="slope")
        nc.vector.tensor_scalar(out=slope[:], in0=gain_col[:], scalar1=float(I), scalar2=r1, op0=ALU.mult, op1=ALU.mult)
        neg_max2 = keep.tile([P, 1], F32, name="neg_max2", tag="listed1", align_bytes=64)
        nc.vector.tensor_scalar(out=neg_max2[:], in0=top[:], scalar1=-float(I), scalar2=r1, op0=ALU.mult, op1=ALU.mult)
        p2 = keep.tile([P, I], F32, name="p2", tag="grouped_w0", align_bytes=64)
        z2 = keep.tile([P, 1], F32, name="z2")
        nc.scalar.activation(out=p2[:], in_=p1[:], func=ACT.Exp, bias=neg_max2[:], scale=slope[:], accum_out=z2[:])
        nc.vector.tensor_copy(listed0[:, :FIRST_ON_VECTOR], pools[0][:].indirect(offsets[:, : FIRST_ON_VECTOR // 16]))
        turned0 = turn_values(listed0, "bank0")
        listed1 = keep.tile([P, I], BF16, name="listed1", tag="listed1", align_bytes=64)
        nc.scalar.activation(listed1[:], pools[1][:].indirect(offsets[:]), ACT.Copy)
        listed2 = keep.tile([P, I], BF16, name="listed2", align_bytes=64)
        nc.scalar.activation(listed2[:], pools[2][:].indirect(offsets[:]), ACT.Copy)

        r2 = keep.tile([P, 1], F32, name="r2")
        nc.vector.reciprocal(r2[:], z2[:])
        w_bf = keep.tile([P, I], BF16, name="w_bf", align_bytes=64)
        nc.vector.scalar_tensor_tensor(out=w_bf[:], in0=p2[:], scalar=r2[:], in1=factor_rows[:].rearrange("q u s e -> q (u s e)"),
                                       op0=ALU.mult, op1=ALU.mult)
        w_words = w_bf[:].bitcast(F32)
        w_turned = turn_pairs([w_words[:, u * P : (u + 1) * P] for u in range(2)], "bank2")
        turned1 = turn_values(listed1, "bank5")
        grouped_w0 = keep.tile([P, 2 * I], BF16, name="grouped_w0", tag="grouped_w0", align_bytes=64)
        interleave(nc.vector.tensor_copy, grouped_w0[:, I:], turned0)
        interleave(nc.vector.tensor_copy, grouped_w0[:, :I], w_turned)
        codes_w0, scales_w0 = quantise("w0", grouped_w0[:], "codes_w0")
        grouped1 = keep.tile([P, I], BF16, name="grouped1", align_bytes=64)
        interleave(nc.vector.tensor_copy, grouped1[:], turned1)
        values1 = quantise("values1", grouped1[:], "codes1")
        turned2 = turn_values(listed2, "bank3")

        listed3 = keep.tile([P, I], BF16, name="listed3", align_bytes=64)
        nc.vector.tensor_copy(listed3[:, :LAST_ON_VECTOR], pools[3][:].indirect(offsets[:, : LAST_ON_VECTOR // 16]))
        nc.scalar.activation(listed3[:, LAST_ON_VECTOR:], pools[3][:].indirect(offsets[:, LAST_ON_VECTOR // 16 :]), ACT.Copy)
        turned3 = turn_values(listed3, "bank4")
        late = keep.tile([P, 2 * half], F32, name="late", tag="pool3", align_bytes=64)
        grouped2 = late[:, half:].bitcast(BF16)
        interleave(nc.scalar.copy, grouped2, turned2)
        values2 = quantise("values2", grouped2, "codes2")
        grouped3 = keep.tile([P, I], BF16, name="grouped3", align_bytes=64)
        interleave(nc.scalar.copy, grouped3[:], turned3)
        values3 = quantise("values3", grouped3[:], "codes3")

        def product(sums, codes, scales):
            nc.tensor.matmul_mx(out=sums, lhsT=codes_w0[:, :P].bitcast(FP8X4), lhsT_scale=scales_w0[:, :P],
                                rhs=codes.bitcast(FP8X4), rhs_scale=scales, start=True, stop=True)

        sums01 = psum.tile([P, 2 * P], F32, name="sums01")
        product(sums01[:, :P], codes_w0[:, P:], scales_w0[:, P:])
        product(sums01[:, P:], values1[0][:], values1[1][:])
        nc.vector.tensor_copy(late[:, :half], sums01[:])
        nc.sync.dma_start(out[:, : 2 * P], late[:, :half])
        sums2 = psum.tile([P, P], F32, name="sums2", tag="bank0")
        product(sums2[:], values2[0][:], values2[1][:])
        result2 = keep.tile([P, P], F32, name="result2")
        nc.vector.tensor_copy(result2[:], sums2[:])
        nc.sync.dma_start(out[:, 2 * P : 3 * P], result2[:])
        sums3 = psum.tile([P, P], F32, name="sums3")
        product(sums3[:], values3[0][:], values3[1][:])
        result3 = keep.tile([P, P], F32, name="result3")
        nc.scalar.copy(result3[:], sums3[:])
        nc.scalar.dma_start(out[:, 3 * P :], result3[:])
